import numpy as np
import ml_dtypes


def mxq(x, axis, fmt="e4m3"):
    dtype, down = {"e4m3": (ml_dtypes.float8_e4m3fn, 7), "e5m2": (ml_dtypes.float8_e5m2, 14)}[fmt]
    v = np.moveaxis(np.asarray(x, np.float32).astype(ml_dtypes.bfloat16).astype(np.float64), axis, -1)
    blocks = v.reshape(v.shape[:-1] + (-1, 32))
    amax = np.abs(blocks).max(-1, keepdims=True)
    byte = np.maximum(np.where(amax > 0, np.frexp(amax)[1] - 1 + 127, 0) - down, 1)
    scale = np.exp2(byte - 127.0)
    codes = (blocks / scale).astype(np.float32).astype(dtype).astype(np.float64)
    return np.moveaxis((codes * scale).reshape(v.shape), -1, axis)


WIDE = False


def mx_kscale(k):
    if not WIDE:
        return np.ones(k)
    levels = np.array([10, -10, 5, -5, 0])
    if k % 512:
        return np.exp2(np.random.permutation(np.resize(levels, k // 32))).repeat(32)
    a = np.empty((k // 512, 16))
    for p in range(k // 512):
        a[p, :8] = np.random.permutation(np.resize(levels, 8))
        for g in range(8):
            far = levels[np.abs(levels - a[p, g]) >= 10]
            a[p, g + 8] = far[np.random.randint(len(far))]
    return np.exp2(a.ravel()).repeat(32)


def f64(x):
    return np.asarray(x).astype(np.float64)


def striped(idx):
    return np.tile(np.asarray(idx).reshape(-1, 16).T, (8, 1)).astype(np.uint16)


def unstriped(offs):
    return offs[:16].T.reshape(-1).astype(np.int64)


E2M1 = np.array([0.0, 0.5, 1.0, 1.5, 2.0, 3.0, 4.0, 6.0, -0.0, -0.5, -1.0, -1.5, -2.0, -3.0, -4.0, -6.0])


def pack_weight(w, fmt):
    k, n = w.shape
    w = f64(np.asarray(w, np.float32).astype(ml_dtypes.bfloat16)).reshape(k // 32, 32, n)
    amax = np.abs(w).max(1)
    if fmt == "e4m3":
        byte = np.frexp(amax)[1] - 1 + 127 - 7
    else:
        mant, ex = np.frexp(amax / 6.0)
        byte = np.where(mant > 0.5, ex, ex - 1) + 127
    byte = np.clip(np.where(amax > 0, byte, 1), 1, 254)
    scaled = (w * np.exp2(127.0 - byte)[:, None, :]).reshape(k, n).astype(np.float32)
    by_word = np.ascontiguousarray(scaled.reshape(k // 512, 128, 4, n).transpose(0, 1, 3, 2))
    if fmt == "e4m3":
        words = by_word.astype(ml_dtypes.float8_e4m3fn).view(np.uint8)
    else:
        c = by_word.astype(ml_dtypes.float4_e2m1fn).view(np.uint8) & 0xF
        words = (c[..., 0::2] | (c[..., 1::2] << 4)).reshape(k // 512, 128, 2 * n)
    return np.ascontiguousarray(words), np.ascontiguousarray(byte.astype(np.uint8).reshape(k // 512, 16, n))


def unpack_weight(words, scales, fmt):
    g, _, n = scales.shape
    words = np.ascontiguousarray(words).reshape(g, 128, n, -1)
    if fmt == "e4m3":
        vals = words.view(ml_dtypes.float8_e4m3fn).astype(np.float64)
    else:
        nib = np.empty((g, 128, n, 4), np.uint8)
        nib[..., 0::2] = words & 0xF
        nib[..., 1::2] = words >> 4
        vals = E2M1[nib]
    vals = vals * np.repeat(np.exp2(scales.astype(np.float64) - 127.0), 8, axis=1)[..., None]
    return vals.transpose(0, 1, 3, 2).reshape(g * 512, n)


D, T, I, Q, E, U, X = 512, 2048, 512, 128, 512, 1024, 1024


def setup_inputs():
    n = np.random.standard_normal
    idx = np.random.permutation(T)[:I]
    idx2 = np.random.permutation(U)[:Q]
    idx3 = np.random.permutation(X)[:I]
    fd = mx_kscale(D)
    fi = mx_kscale(I)
    keysp = pack_weight(n((D, T)) / fd[:, None], "e4m3")
    return {
        "users": (n((D, U)) * 1.0 / np.sqrt(D) * fd[:, None]).astype(np.float32),
        "keys_words": keysp[0],
        "keys_scales": keysp[1],
        "os": (np.random.uniform(0.02, 0.08, (1, I)) * fi).astype(np.float32),
        "vals": (n((E, T))).astype(np.float32),
        "vals2": (n((E, X))).astype(np.float32),
        "vsc": (np.random.uniform(0.5, 2.0, (1, I)) / fi).astype(np.float32),
        "offs": striped(idx),
        "offs2": striped(idx2),
        "offs3": striped(idx3),
    }


def reference(users, keys_words, keys_scales, os, vals, vals2, vsc, offs, offs2, offs3):
    idx = unstriped(offs)
    idx2 = unstriped(offs2)
    idx3 = unstriped(offs3)
    keysu = unpack_weight(keys_words, keys_scales, "e4m3")
    usersidx2q = mxq(f64(users)[:, idx2], 0, "e4m3")
    keysidxg = keysu[:, idx]
    w = usersidx2q.T @ keysidxg
    wo1 = w * f64(os)
    wt1 = wo1.T
    vz = np.maximum(f64(vals)[:, idx], f64(vals2)[:, idx3]) * f64(vsc)
    vt1 = vz.T
    wt1q = mxq(wt1, 0, "e4m3")
    vt1q = mxq(vt1, 0, "e4m3")
    o = wt1q.T @ vt1q
    return o

@@ -1,0 +1,189 @@
+from contextlib import ExitStack
+
+import concourse.mybir as mybir
+from concourse.masks import make_identity
+
+D, T, I, Q, E, U, X = 512, 2048, 512, 128, 512, 1024, 1024
+FLOPS = 2 * D * Q * I + 2 * I * Q * E
+
+F32 = mybir.dt.float32
+BF16 = mybir.dt.bfloat16
+I32 = mybir.dt.int32
+U32 = mybir.dt.uint32
+U16 = mybir.dt.uint16
+U8 = mybir.dt.uint8
+FP8X4 = mybir.dt.float8_e4m3fn_x4
+COPY = mybir.ActivationFunctionType.Copy
+MULT = mybir.AluOpType.mult
+MAX = mybir.AluOpType.max
+
+P = 128
+PACK = 4
+RUN = 8
+BLOCKS = I // (PACK * RUN)
+E_TILES = E // P
+HALF = I // 2
+LIST_COLS = I // 16
+
+
+def tile_attend_listedqueries_mergedvalues_lean_kernel(
+    tc, users, keys_words, keys_scales, wsc, vals, vals2, vsc, offs, offs2, offs3, out
+):
+    nc = tc.nc
+
+    def dealt(tile):
+        return tile[:].rearrange("p t (b j) -> p b t j", j=RUN)
+
+    def listed(ap):
+        return ap.rearrange("p (b t j) -> p b t j", t=PACK, j=RUN)
+
+    with ExitStack() as ctx:
+        lists = ctx.enter_context(tc.tile_pool(name="lists", bufs=1))
+        held = ctx.enter_context(tc.tile_pool(name="held", bufs=1))
+        ring = ctx.enter_context(tc.tile_pool(name="ring", bufs=4))
+        psum = ctx.enter_context(tc.psum_pool(name="psum", bufs=1))
+        turn = ctx.enter_context(tc.psum_pool(name="turn", bufs=4))
+
+        idx = lists.tile([P, LIST_COLS], U16, name="idx")
+        idx2 = lists.tile([P, Q // 16], U16, name="idx2")
+        idx3 = lists.tile([P, LIST_COLS], U16, name="idx3")
+
+        key_words = held.tile([P, T], I32, name="key_words")
+        key_scales = held.tile([P, T], U8, name="key_scales")
+        factor_rows = held.tile([P, P], F32, name="factor_rows")
+        identity = held.tile([P, P], F32, name="identity")
+        user_planes = held.tile([P, PACK, U], F32, name="user_planes")
+        scale_stage = held.tile([P, 2, T // 4], I32, name="scale_stage")
+        factor_stage = held.tile([2 * PACK, P], F32, name="factor_stage")
+        first = [held.tile([P, T], F32, name=f"first{e}") for e in range(E_TILES)]
+        second = [held.tile([P, X], F32, name=f"second{e}") for e in range(E_TILES)]
+
+        nc.vector.memset(key_scales[:].bitcast(I32), 0)
+        nc.vector.memset(factor_rows[:], 0.0)
+        make_identity(nc, identity[:])
+
+        nc.sync.dma_start(key_words[:], keys_words[0].rearrange("p n t -> p (n t)").bitcast(I32))
+        nc.sync.dma_start(idx[:], offs)
+        scale_rows = keys_scales[0].bitcast(I32).rearrange("(h g r) w -> h r g w", h=2, g=2)
+        for h in range(2):
+            nc.sync.dma_start(scale_stage[64 * h : 64 * h + 4], scale_rows[h])
+        nc.sync.dma_start(user_planes[:], users.rearrange("(p t) u -> p t u", t=PACK))
+        nc.sync.dma_start(idx2[:], offs2)
+        for row, factor in ((0, wsc), (PACK, vsc)):
+            nc.sync.dma_start(
+                factor_stage[row : row + PACK, :].rearrange("t (b j) -> t b j", j=RUN),
+                factor.rearrange("o (b t j) -> t (o b) j", t=PACK, j=RUN),
+            )
+        for e in range(E_TILES):
+            nc.sync.dma_start(second[e][:], vals2[e * P : (e + 1) * P, :])
+            if e == 0:
+                nc.sync.dma_start(idx3[:], offs3)
+            nc.sync.dma_start(first[e][:], vals[e * P : (e + 1) * P, :])
+
+        for quad in range(4):
+            source = 64 * (quad // 2)
+            nc.vector.tensor_copy(
+                key_scales[32 * quad : 32 * quad + 4, :].bitcast(I32),
+                scale_stage[source : source + 4, quad % 2, :],
+            )
+        nc.vector.tensor_copy(factor_rows[: 2 * PACK, :], factor_stage[:])
+
+        factor_bank = psum.tile([P, P], F32, name="factor_bank")
+        nc.tensor.transpose(factor_bank[:], factor_rows[:], identity[:])
+        factors = held.tile([P, 2 * PACK], F32, name="factors")
+        nc.scalar.activation(factors[:], factor_bank[:, : 2 * PACK], COPY)
+
+        picked_words = held.tile([P, PACK, P], U32, name="picked_words", align_bytes=64)
+        picked_scales = held.tile([P, PACK, P], U8, name="picked_scales", align_bytes=64)
+        nc.vector.tensor_copy(dealt(picked_words), key_words[:].bitcast(U32).indirect(idx[:]))
+        nc.vector.tensor_copy(dealt(picked_scales), key_scales[:].indirect(idx[:]))
+
+        queries = held.tile([P, Q, PACK], BF16, name="queries", align_bytes=64)
+        for t in range(PACK):
+            nc.vector.tensor_copy(queries[:, :, t], user_planes[:, t, :].indirect(idx2[:]))
+        query_codes = held.tile([P, Q], U32, name="query_codes", align_bytes=64)
+        query_scales = held.tile([P, Q], U8, name="query_scales", align_bytes=64)
+        nc.vector.quantize_mx(
+            out=query_codes[:].bitcast(FP8X4),
+            scales=query_scales[:],
+            in_=queries[:].rearrange("p q t -> p (q t)"),
+        )
+
+        score_bank = psum.tile([P, PACK, Q], F32, name="score_bank")
+        for t in range(PACK):
+            nc.tensor.matmul_mx(
+                out=score_bank[:, t, :],
+                lhsT=picked_words[:, t, :].bitcast(FP8X4),
+                lhsT_scale=picked_scales[:, t, :],
+                rhs=query_codes[:].bitcast(FP8X4),
+                rhs_scale=query_scales[:],
+                start=True,
+                stop=True,
+            )
+        weights = held.tile([P, Q, PACK], BF16, name="weights", align_bytes=64)
+        nc.vector.tensor_tensor(
+            weights[:],
+            score_bank[:].rearrange("p t q -> p q t"),
+            factors[:, 0:PACK].unsqueeze(1).to_broadcast([P, Q, PACK]),
+            MULT,
+        )
+        weight_codes = held.tile([P, Q], U32, name="weight_codes", align_bytes=64)
+        weight_scales = held.tile([P, Q], U8, name="weight_scales", align_bytes=64)
+        nc.vector.quantize_mx(
+            out=weight_codes[:].bitcast(FP8X4),
+            scales=weight_scales[:],
+            in_=weights[:].rearrange("p q t -> p (q t)"),
+        )
+
+        early_bank = psum.tile([P, E - P], F32, name="early_bank")
+        last_bank = psum.tile([P, P], F32, name="last_bank")
+        for e in range(E_TILES):
+            picked_second = ring.tile([P, I], F32, name="picked_second")
+            nc.scalar.activation(picked_second[:], second[e][:].indirect(idx3[:]), COPY)
+            picked_low = ring.tile([P, HALF], F32, name="picked_low")
+            picked_high = ring.tile([P, HALF], F32, name="picked_high")
+            nc.vector.tensor_copy(picked_low[:], first[e][:].indirect(idx[:, : LIST_COLS // 2]))
+            nc.scalar.activation(picked_high[:], first[e][:].indirect(idx[:, LIST_COLS // 2 :]), COPY)
+
+            larger = ring.tile([P, PACK, P], F32, name="larger")
+            for h, picked_first in enumerate((picked_low, picked_high)):
+                nc.vector.tensor_tensor(
+                    dealt(larger)[:, h * BLOCKS // 2 : (h + 1) * BLOCKS // 2],
+                    listed(picked_first[:]),
+                    listed(picked_second[:, h * HALF : (h + 1) * HALF]),
+                    MAX,
+                )
+            turned = turn.tile([P, PACK, P], F32, name="turned")
+            for t in range(PACK):
+                nc.tensor.transpose(turned[:, t, :], larger[:, t, :], identity[:])
+            values = ring.tile([P, P, PACK], BF16, name="values", align_bytes=64)
+            nc.vector.tensor_tensor(
+                values[:],
+                turned[:].rearrange("p t e -> p e t"),
+                factors[:, PACK : 2 * PACK].unsqueeze(1).to_broadcast([P, P, PACK]),
+                MULT,
+            )
+            value_codes = ring.tile([P, P], U32, name="value_codes", align_bytes=64)
+            value_scales = ring.tile([P, P], U8, name="value_scales", align_bytes=64)
+            nc.vector.quantize_mx(
+                out=value_codes[:].bitcast(FP8X4),
+                scales=value_scales[:],
+                in_=values[:].rearrange("p e t -> p (e t)"),
+            )
+            last = e == E_TILES - 1
+            nc.tensor.matmul_mx(
+                out=last_bank[:] if last else early_bank[:, e * P : (e + 1) * P],
+                lhsT=weight_codes[:].bitcast(FP8X4),
+                lhsT_scale=weight_scales[:],
+                rhs=value_codes[:].bitcast(FP8X4),
+                rhs_scale=value_scales[:],
+                start=True,
+                stop=True,
+            )
+
+        early = held.tile([P, E - P], F32, name="early", tag=f"first{E_TILES - 1}")
+        nc.scalar.activation(early[:], early_bank[:], COPY)
+        nc.sync.dma_start(out[:, : E - P], early[:])
+        late = held.tile([P, P], F32, name="late")
+        nc.scalar.activation(late[:], last_bank[:], COPY)
+        nc.sync.dma_start(out[:, E - P :], late[:])

@@ -52,7 +52,7 @@ def tile_attend_listedqueries_mergedvalues_lean_kernel(
         key_scales = held.tile([P, T], U8, name="key_scales")
         factor_rows = held.tile([P, P], F32, name="factor_rows")
         identity = held.tile([P, P], F32, name="identity")
-        user_planes = held.tile([P, PACK, U], F32, name="user_planes")
+        user_planes = [held.tile([P, U], F32, name=f"user_plane{t}") for t in range(PACK)]
         scale_stage = held.tile([P, 2, T // 4], I32, name="scale_stage")
         factor_stage = held.tile([2 * PACK, P], F32, name="factor_stage")
         first = [held.tile([P, T], F32, name=f"first{e}") for e in range(E_TILES)]
@@ -67,17 +67,24 @@ def tile_attend_listedqueries_mergedvalues_lean_kernel(
         scale_rows = keys_scales[0].bitcast(I32).rearrange("(h g r) w -> h r g w", h=2, g=2)
         for h in range(2):
             nc.sync.dma_start(scale_stage[64 * h : 64 * h + 4], scale_rows[h])
-        nc.sync.dma_start(user_planes[:], users.rearrange("(p t) u -> p t u", t=PACK))
-        nc.sync.dma_start(idx2[:], offs2)
-        for row, factor in ((0, wsc), (PACK, vsc)):
+        user_rows = users.rearrange("(p t) u -> t p u", t=PACK)
+
+        def load_factor(row, factor):
             nc.sync.dma_start(
                 factor_stage[row : row + PACK, :].rearrange("t (b j) -> t b j", j=RUN),
                 factor.rearrange("o (b t j) -> t (o b) j", t=PACK, j=RUN),
             )
+
+        nc.sync.dma_start(user_planes[0][:], user_rows[0])
+        nc.sync.dma_start(idx2[:], offs2)
+        nc.sync.dma_start(user_planes[1][:], user_rows[1])
+        load_factor(0, wsc)
+        nc.sync.dma_start(user_planes[2][:], user_rows[2])
+        load_factor(PACK, vsc)
+        nc.sync.dma_start(user_planes[3][:], user_rows[3])
+        nc.sync.dma_start(idx3[:], offs3)
         for e in range(E_TILES):
             nc.sync.dma_start(second[e][:], vals2[e * P : (e + 1) * P, :])
-            if e == 0:
-                nc.sync.dma_start(idx3[:], offs3)
             nc.sync.dma_start(first[e][:], vals[e * P : (e + 1) * P, :])
 
         for quad in range(4):
@@ -99,8 +106,10 @@ def tile_attend_listedqueries_mergedvalues_lean_kernel(
         nc.vector.tensor_copy(dealt(picked_scales), key_scales[:].indirect(idx[:]))
 
         queries = held.tile([P, Q, PACK], BF16, name="queries", align_bytes=64)
+        picked_users = held.tile([P, PACK, Q], BF16, name="picked_users")
         for t in range(PACK):
-            nc.vector.tensor_copy(queries[:, :, t], user_planes[:, t, :].indirect(idx2[:]))
+            nc.scalar.activation(picked_users[:, t, :], user_planes[t][:].indirect(idx2[:]), COPY)
+        nc.vector.tensor_copy(queries[:], picked_users[:].rearrange("p t q -> p q t"))
         query_codes = held.tile([P, Q], U32, name="query_codes", align_bytes=64)
         query_scales = held.tile([P, Q], U8, name="query_scales", align_bytes=64)
         nc.vector.quantize_mx(
@@ -137,14 +146,14 @@ def tile_attend_listedqueries_mergedvalues_lean_kernel(
 
         early_bank = psum.tile([P, E - P], F32, name="early_bank")
         last_bank = psum.tile([P, P], F32, name="last_bank")
-        for e in range(E_TILES):
+
+        def merge_and_turn(e):
             picked_second = ring.tile([P, I], F32, name="picked_second")
             nc.scalar.activation(picked_second[:], second[e][:].indirect(idx3[:]), COPY)
-            picked_low = ring.tile([P, HALF], F32, name="picked_low")
+            picked_low = held.tile([P, HALF], F32, name="picked_low", tag="turnstile", align_bytes=64)
             picked_high = ring.tile([P, HALF], F32, name="picked_high")
             nc.vector.tensor_copy(picked_low[:], first[e][:].indirect(idx[:, : LIST_COLS // 2]))
             nc.scalar.activation(picked_high[:], first[e][:].indirect(idx[:, LIST_COLS // 2 :]), COPY)
-
             larger = ring.tile([P, PACK, P], F32, name="larger")
             for h, picked_first in enumerate((picked_low, picked_high)):
                 nc.vector.tensor_tensor(
@@ -156,7 +165,10 @@ def tile_attend_listedqueries_mergedvalues_lean_kernel(
             turned = turn.tile([P, PACK, P], F32, name="turned")
             for t in range(PACK):
                 nc.tensor.transpose(turned[:, t, :], larger[:, t, :], identity[:])
-            values = ring.tile([P, P, PACK], BF16, name="values", align_bytes=64)
+            return turned
+
+        def scale_and_multiply(e, turned):
+            values = held.tile([P, P, PACK], BF16, name="values", tag="turnstile", align_bytes=64)
             nc.vector.tensor_tensor(
                 values[:],
                 turned[:].rearrange("p t e -> p e t"),
@@ -170,9 +182,8 @@ def tile_attend_listedqueries_mergedvalues_lean_kernel(
                 scales=value_scales[:],
                 in_=values[:].rearrange("p e t -> p (e t)"),
             )
-            last = e == E_TILES - 1
             nc.tensor.matmul_mx(
-                out=last_bank[:] if last else early_bank[:, e * P : (e + 1) * P],
+                out=last_bank[:] if e == E_TILES - 1 else early_bank[:, e * P : (e + 1) * P],
                 lhsT=weight_codes[:].bitcast(FP8X4),
                 lhsT_scale=weight_scales[:],
                 rhs=value_codes[:].bitcast(FP8X4),
@@ -181,9 +192,15 @@ def tile_attend_listedqueries_mergedvalues_lean_kernel(
                 stop=True,
             )
 
-        early = held.tile([P, E - P], F32, name="early", tag=f"first{E_TILES - 1}")
+        turned = merge_and_turn(0)
+        for e in range(1, E_TILES):
+            ahead = merge_and_turn(e)
+            scale_and_multiply(e - 1, turned)
+            turned = ahead
+        early = held.tile([P, E - P], F32, name="early")
         nc.scalar.activation(early[:], early_bank[:], COPY)
         nc.sync.dma_start(out[:, : E - P], early[:])
+        scale_and_multiply(E_TILES - 1, turned)
         late = held.tile([P, P], F32, name="late")
         nc.scalar.activation(late[:], last_bank[:], COPY)
         nc.sync.dma_start(out[:, E - P :], late[:])

@@ -50,11 +50,11 @@ def tile_attend_listedqueries_mergedvalues_lean_kernel(
 
         key_words = held.tile([P, T], I32, name="key_words")
         key_scales = held.tile([P, T], U8, name="key_scales")
-        factor_rows = held.tile([P, P], F32, name="factor_rows")
+        factor_rows = held.tile([P, PACK, P], F32, name="factor_rows")
         identity = held.tile([P, P], F32, name="identity")
-        user_planes = [held.tile([P, U], F32, name=f"user_plane{t}") for t in range(PACK)]
-        scale_stage = held.tile([P, 2, T // 4], I32, name="scale_stage")
-        factor_stage = held.tile([2 * PACK, P], F32, name="factor_stage")
+        user_planes = held.tile([P, PACK, U], F32, name="user_planes")
+        scale_stage = held.tile([P, T // 4], I32, name="scale_stage")
+        factor_stage = held.tile([2, I], F32, name="factor_stage")
         first = [held.tile([P, T], F32, name=f"first{e}") for e in range(E_TILES)]
         second = [held.tile([P, X], F32, name=f"second{e}") for e in range(E_TILES)]
 
@@ -62,53 +62,41 @@ def tile_attend_listedqueries_mergedvalues_lean_kernel(
         nc.vector.memset(factor_rows[:], 0.0)
         make_identity(nc, identity[:])
 
+        nc.sync.dma_start(user_planes[:], users.rearrange("(p t) u -> p t u", t=PACK))
+        nc.sync.dma_start(idx2[:], offs2)
+        scale_rows = keys_scales[0].bitcast(I32).rearrange("(quad r) w -> r quad w", r=4)
+        for r in range(4):
+            nc.sync.dma_start(scale_stage[r:P:32, :], scale_rows[r])
         nc.sync.dma_start(key_words[:], keys_words[0].rearrange("p n t -> p (n t)").bitcast(I32))
         nc.sync.dma_start(idx[:], offs)
-        scale_rows = keys_scales[0].bitcast(I32).rearrange("(h g r) w -> h r g w", h=2, g=2)
-        for h in range(2):
-            nc.sync.dma_start(scale_stage[64 * h : 64 * h + 4], scale_rows[h])
-        user_rows = users.rearrange("(p t) u -> t p u", t=PACK)
-
-        def load_factor(row, factor):
-            nc.sync.dma_start(
-                factor_stage[row : row + PACK, :].rearrange("t (b j) -> t b j", j=RUN),
-                factor.rearrange("o (b t j) -> t (o b) j", t=PACK, j=RUN),
-            )
-
-        nc.sync.dma_start(user_planes[0][:], user_rows[0])
-        nc.sync.dma_start(idx2[:], offs2)
-        nc.sync.dma_start(user_planes[1][:], user_rows[1])
-        load_factor(0, wsc)
-        nc.sync.dma_start(user_planes[2][:], user_rows[2])
-        load_factor(PACK, vsc)
-        nc.sync.dma_start(user_planes[3][:], user_rows[3])
-        nc.sync.dma_start(idx3[:], offs3)
         for e in range(E_TILES):
             nc.sync.dma_start(second[e][:], vals2[e * P : (e + 1) * P, :])
+            if e == 0:
+                nc.sync.dma_start(factor_stage[0:1, :], wsc)
+                nc.sync.dma_start(factor_stage[1:2, :], vsc)
+                nc.sync.dma_start(idx3[:], offs3)
             nc.sync.dma_start(first[e][:], vals[e * P : (e + 1) * P, :])
 
         for quad in range(4):
-            source = 64 * (quad // 2)
-            nc.vector.tensor_copy(
-                key_scales[32 * quad : 32 * quad + 4, :].bitcast(I32),
-                scale_stage[source : source + 4, quad % 2, :],
-            )
-        nc.vector.tensor_copy(factor_rows[: 2 * PACK, :], factor_stage[:])
+            rows = slice(32 * quad, 32 * quad + 4)
+            nc.vector.tensor_copy(key_scales[rows, :].bitcast(I32), scale_stage[rows, :])
 
-        factor_bank = psum.tile([P, P], F32, name="factor_bank")
-        nc.tensor.transpose(factor_bank[:], factor_rows[:], identity[:])
-        factors = held.tile([P, 2 * PACK], F32, name="factors")
-        nc.scalar.activation(factors[:], factor_bank[:, : 2 * PACK], COPY)
+        nc.vector.tensor_copy(dealt(factor_rows)[0:2], listed(factor_stage[:]))
+        factor_bank = psum.tile([P, PACK, P], F32, name="factor_bank")
+        for t in range(PACK):
+            nc.tensor.transpose(factor_bank[:, t, :], factor_rows[:, t, :], identity[:])
+        factors = held.tile([P, 2, PACK], F32, name="factors")
+        nc.scalar.activation(factors[:], factor_bank[:, :, 0:2].rearrange("p t s -> p s t"), COPY)
 
         picked_words = held.tile([P, PACK, P], U32, name="picked_words", align_bytes=64)
         picked_scales = held.tile([P, PACK, P], U8, name="picked_scales", align_bytes=64)
-        nc.vector.tensor_copy(dealt(picked_words), key_words[:].bitcast(U32).indirect(idx[:]))
         nc.vector.tensor_copy(dealt(picked_scales), key_scales[:].indirect(idx[:]))
+        nc.vector.tensor_copy(dealt(picked_words), key_words[:].bitcast(U32).indirect(idx[:]))
 
         queries = held.tile([P, Q, PACK], BF16, name="queries", align_bytes=64)
-        picked_users = held.tile([P, PACK, Q], BF16, name="picked_users")
+        picked_users = held.tile([P, PACK, Q], F32, name="picked_users")
         for t in range(PACK):
-            nc.scalar.activation(picked_users[:, t, :], user_planes[t][:].indirect(idx2[:]), COPY)
+            nc.scalar.activation(picked_users[:, t, :], user_planes[:, t, :].indirect(idx2[:]), COPY)
         nc.vector.tensor_copy(queries[:], picked_users[:].rearrange("p t q -> p q t"))
         query_codes = held.tile([P, Q], U32, name="query_codes", align_bytes=64)
         query_scales = held.tile([P, Q], U8, name="query_scales", align_bytes=64)
@@ -133,7 +121,7 @@ def tile_attend_listedqueries_mergedvalues_lean_kernel(
         nc.vector.tensor_tensor(
             weights[:],
             score_bank[:].rearrange("p t q -> p q t"),
-            factors[:, 0:PACK].unsqueeze(1).to_broadcast([P, Q, PACK]),
+            factors[:, 0:1, :].to_broadcast([P, Q, PACK]),
             MULT,
         )
         weight_codes = held.tile([P, Q], U32, name="weight_codes", align_bytes=64)
@@ -172,7 +160,7 @@ def tile_attend_listedqueries_mergedvalues_lean_kernel(
             nc.vector.tensor_tensor(
                 values[:],
                 turned[:].rearrange("p t e -> p e t"),
-                factors[:, PACK : 2 * PACK].unsqueeze(1).to_broadcast([P, P, PACK]),
+                factors[:, 1:2, :].to_broadcast([P, P, PACK]),
                 MULT,
             )
             value_codes = ring.tile([P, P], U32, name="value_codes", align_bytes=64)

@@ -42,7 +42,7 @@ def tile_attend_listedqueries_mergedvalues_lean_kernel(
         held = ctx.enter_context(tc.tile_pool(name="held", bufs=1))
         ring = ctx.enter_context(tc.tile_pool(name="ring", bufs=4))
         psum = ctx.enter_context(tc.psum_pool(name="psum", bufs=1))
-        turn = ctx.enter_context(tc.psum_pool(name="turn", bufs=4))
+        turn = ctx.enter_context(tc.psum_pool(name="turn", bufs=3))
 
         idx = lists.tile([P, LIST_COLS], U16, name="idx")
         idx2 = lists.tile([P, Q // 16], U16, name="idx2")
@@ -50,53 +50,53 @@ def tile_attend_listedqueries_mergedvalues_lean_kernel(
 
         key_words = held.tile([P, T], I32, name="key_words")
         key_scales = held.tile([P, T], U8, name="key_scales")
-        factor_rows = held.tile([P, PACK, P], F32, name="factor_rows")
         identity = held.tile([P, P], F32, name="identity")
-        user_planes = held.tile([P, PACK, U], F32, name="user_planes")
+        user_pairs = [held.tile([P, 2, U], F32, name=f"user_pair{u}") for u in range(2)]
         scale_stage = held.tile([P, T // 4], I32, name="scale_stage")
         factor_stage = held.tile([2, I], F32, name="factor_stage")
         first = [held.tile([P, T], F32, name=f"first{e}") for e in range(E_TILES)]
         second = [held.tile([P, X], F32, name=f"second{e}") for e in range(E_TILES)]
 
         nc.vector.memset(key_scales[:].bitcast(I32), 0)
-        nc.vector.memset(factor_rows[:], 0.0)
         make_identity(nc, identity[:])
 
-        nc.sync.dma_start(user_planes[:], users.rearrange("(p t) u -> p t u", t=PACK))
-        nc.sync.dma_start(idx2[:], offs2)
+        user_rows = users.rearrange("(p u v) c -> u p v c", u=2, v=2)
         scale_rows = keys_scales[0].bitcast(I32).rearrange("(quad r) w -> r quad w", r=4)
-        for r in range(4):
-            nc.sync.dma_start(scale_stage[r:P:32, :], scale_rows[r])
         nc.sync.dma_start(key_words[:], keys_words[0].rearrange("p n t -> p (n t)").bitcast(I32))
         nc.sync.dma_start(idx[:], offs)
+        for r in range(4):
+            nc.sync.dma_start(scale_stage[r:P:32, :], scale_rows[r])
+        nc.sync.dma_start(idx2[:], offs2)
+        for u in range(2):
+            nc.sync.dma_start(user_pairs[u][:], user_rows[u])
+        nc.sync.dma_start(factor_stage[0:1, :], wsc)
+        nc.sync.dma_start(factor_stage[1:2, :], vsc)
+        nc.sync.dma_start(idx3[:], offs3)
         for e in range(E_TILES):
             nc.sync.dma_start(second[e][:], vals2[e * P : (e + 1) * P, :])
-            if e == 0:
-                nc.sync.dma_start(factor_stage[0:1, :], wsc)
-                nc.sync.dma_start(factor_stage[1:2, :], vsc)
-                nc.sync.dma_start(idx3[:], offs3)
             nc.sync.dma_start(first[e][:], vals[e * P : (e + 1) * P, :])
 
         for quad in range(4):
             rows = slice(32 * quad, 32 * quad + 4)
             nc.vector.tensor_copy(key_scales[rows, :].bitcast(I32), scale_stage[rows, :])
-
-        nc.vector.tensor_copy(dealt(factor_rows)[0:2], listed(factor_stage[:]))
-        factor_bank = psum.tile([P, PACK, P], F32, name="factor_bank")
-        for t in range(PACK):
-            nc.tensor.transpose(factor_bank[:, t, :], factor_rows[:, t, :], identity[:])
-        factors = held.tile([P, 2, PACK], F32, name="factors")
-        nc.scalar.activation(factors[:], factor_bank[:, :, 0:2].rearrange("p t s -> p s t"), COPY)
-
         picked_words = held.tile([P, PACK, P], U32, name="picked_words", align_bytes=64)
         picked_scales = held.tile([P, PACK, P], U8, name="picked_scales", align_bytes=64)
         nc.vector.tensor_copy(dealt(picked_scales), key_scales[:].indirect(idx[:]))
         nc.vector.tensor_copy(dealt(picked_words), key_words[:].bitcast(U32).indirect(idx[:]))
 
+        factor_rows = held.tile([P, PACK, P], F32, name="factor_rows", tag="key_words")
+        nc.vector.memset(factor_rows[:], 0.0)
+        nc.vector.tensor_copy(dealt(factor_rows)[0:2], listed(factor_stage[:]))
+        factor_bank = psum.tile([P, PACK, P], F32, name="factor_bank")
+        for t in range(PACK):
+            nc.tensor.transpose(factor_bank[:, t, :], factor_rows[:, t, :], identity[:])
+        factors = held.tile([P, 2, PACK], F32, name="factors")
+        nc.vector.tensor_copy(factors[:], factor_bank[:, :, 0:2].rearrange("p t s -> p s t"))
+
         queries = held.tile([P, Q, PACK], BF16, name="queries", align_bytes=64)
         picked_users = held.tile([P, PACK, Q], F32, name="picked_users")
         for t in range(PACK):
-            nc.scalar.activation(picked_users[:, t, :], user_planes[:, t, :].indirect(idx2[:]), COPY)
+            nc.scalar.activation(picked_users[:, t, :], user_pairs[t // 2][:, t % 2, :].indirect(idx2[:]), COPY)
         nc.vector.tensor_copy(queries[:], picked_users[:].rearrange("p t q -> p q t"))
         query_codes = held.tile([P, Q], U32, name="query_codes", align_bytes=64)
         query_scales = held.tile([P, Q], U8, name="query_scales", align_bytes=64)
@@ -132,8 +132,8 @@ def tile_attend_listedqueries_mergedvalues_lean_kernel(
             in_=weights[:].rearrange("p q t -> p (q t)"),
         )
 
-        early_bank = psum.tile([P, E - P], F32, name="early_bank")
-        last_bank = psum.tile([P, P], F32, name="last_bank")
+        early_bank = psum.tile([P, 2 * P], F32, name="early_bank")
+        late_banks = [psum.tile([P, P], F32, name=f"late_bank{e}") for e in range(2)]
 
         def merge_and_turn(e):
             picked_second = ring.tile([P, I], F32, name="picked_second")
@@ -143,11 +143,15 @@ def tile_attend_listedqueries_mergedvalues_lean_kernel(
             nc.vector.tensor_copy(picked_low[:], first[e][:].indirect(idx[:, : LIST_COLS // 2]))
             nc.scalar.activation(picked_high[:], first[e][:].indirect(idx[:, LIST_COLS // 2 :]), COPY)
             larger = ring.tile([P, PACK, P], F32, name="larger")
-            for h, picked_first in enumerate((picked_low, picked_high)):
+            low, high = slice(0, BLOCKS // 2), slice(BLOCKS // 2, BLOCKS)
+            nc.vector.tensor_tensor(
+                dealt(larger)[:, low], listed(picked_low[:]), listed(picked_second[:])[:, low], MAX
+            )
+            for places in (slice(0, 2), slice(2, 4)):
                 nc.vector.tensor_tensor(
-                    dealt(larger)[:, h * BLOCKS // 2 : (h + 1) * BLOCKS // 2],
-                    listed(picked_first[:]),
-                    listed(picked_second[:, h * HALF : (h + 1) * HALF]),
+                    dealt(larger)[:, high, places],
+                    listed(picked_high[:])[:, :, places],
+                    listed(picked_second[:])[:, high, places],
                     MAX,
                 )
             turned = turn.tile([P, PACK, P], F32, name="turned")
@@ -171,7 +175,7 @@ def tile_attend_listedqueries_mergedvalues_lean_kernel(
                 in_=values[:].rearrange("p e t -> p (e t)"),
             )
             nc.tensor.matmul_mx(
-                out=last_bank[:] if e == E_TILES - 1 else early_bank[:, e * P : (e + 1) * P],
+                out=early_bank[:, e * P : (e + 1) * P] if e < 2 else late_banks[e - 2][:],
                 lhsT=weight_codes[:].bitcast(FP8X4),
                 lhsT_scale=weight_scales[:],
                 rhs=value_codes[:].bitcast(FP8X4),
@@ -185,10 +189,11 @@ def tile_attend_listedqueries_mergedvalues_lean_kernel(
             ahead = merge_and_turn(e)
             scale_and_multiply(e - 1, turned)
             turned = ahead
-        early = held.tile([P, E - P], F32, name="early")
-        nc.scalar.activation(early[:], early_bank[:], COPY)
-        nc.sync.dma_start(out[:, : E - P], early[:])
         scale_and_multiply(E_TILES - 1, turned)
-        late = held.tile([P, P], F32, name="late")
-        nc.scalar.activation(late[:], last_bank[:], COPY)
-        nc.sync.dma_start(out[:, E - P :], late[:])
+        early = held.tile([P, 2 * P], F32, name="early", tag=f"first{E_TILES - 1}")
+        nc.scalar.activation(early[:], early_bank[:], COPY)
+        nc.sync.dma_start(out[:, : 2 * P], early[:])
+        for e in range(2, E_TILES):
+            late = ring.tile([P, P], F32, name="late")
+            nc.scalar.activation(late[:], late_banks[e - 2][:], COPY)
+            nc.sync.dma_start(out[:, e * P : (e + 1) * P], late[:])

@@ -66,11 +66,11 @@ def tile_attend_listedqueries_mergedvalues_lean_kernel(
         nc.sync.dma_start(idx[:], offs)
         for r in range(4):
             nc.sync.dma_start(scale_stage[r:P:32, :], scale_rows[r])
-        nc.sync.dma_start(idx2[:], offs2)
-        for u in range(2):
-            nc.sync.dma_start(user_pairs[u][:], user_rows[u])
         nc.sync.dma_start(factor_stage[0:1, :], wsc)
+        nc.sync.dma_start(user_pairs[0][:], user_rows[0])
         nc.sync.dma_start(factor_stage[1:2, :], vsc)
+        nc.sync.dma_start(idx2[:], offs2)
+        nc.sync.dma_start(user_pairs[1][:], user_rows[1])
         nc.sync.dma_start(idx3[:], offs3)
         for e in range(E_TILES):
             nc.sync.dma_start(second[e][:], vals2[e * P : (e + 1) * P, :])
@@ -160,14 +160,16 @@ def tile_attend_listedqueries_mergedvalues_lean_kernel(
             return turned
 
         def scale_and_multiply(e, turned):
-            values = held.tile([P, P, PACK], BF16, name="values", tag="turnstile", align_bytes=64)
+            tag = "turnstile" if e < E_TILES - 2 else f"values{e}"
+            values = held.tile([P, P, PACK], BF16, name="values", tag=tag, align_bytes=64)
             nc.vector.tensor_tensor(
                 values[:],
                 turned[:].rearrange("p t e -> p e t"),
                 factors[:, 1:2, :].to_broadcast([P, P, PACK]),
                 MULT,
             )
-            value_codes = ring.tile([P, P], U32, name="value_codes", align_bytes=64)
+            tag = "turnstile" if e == E_TILES - 2 else f"value_codes{e}"
+            value_codes = held.tile([P, P], U32, name="value_codes", tag=tag, align_bytes=64)
             value_scales = ring.tile([P, P], U8, name="value_scales", align_bytes=64)
             nc.vector.quantize_mx(
                 out=value_codes[:].bitcast(FP8X4),

from contextlib import ExitStack

import concourse.mybir as mybir
from concourse.masks import make_identity

D, T, I, Q, E, U, X = 512, 2048, 512, 128, 512, 1024, 1024
FLOPS = 2 * D * Q * I + 2 * I * Q * E

F32 = mybir.dt.float32
BF16 = mybir.dt.bfloat16
I32 = mybir.dt.int32
U32 = mybir.dt.uint32
U16 = mybir.dt.uint16
U8 = mybir.dt.uint8
FP8X4 = mybir.dt.float8_e4m3fn_x4
COPY = mybir.ActivationFunctionType.Copy
MULT = mybir.AluOpType.mult
MAX = mybir.AluOpType.max

P = 128
PACK = 4
RUN = 8
BLOCKS = I // (PACK * RUN)
E_TILES = E // P
HALF = I // 2
LIST_COLS = I // 16


def tile_attend_listedqueries_mergedvalues_lean_kernel(
    tc, users, keys_words, keys_scales, wsc, vals, vals2, vsc, offs, offs2, offs3, out
):
    nc = tc.nc

    def dealt(tile):
        return tile[:].rearrange("p t (b j) -> p b t j", j=RUN)

    def listed(ap):
        return ap.rearrange("p (b t j) -> p b t j", t=PACK, j=RUN)

    with ExitStack() as ctx:
        lists = ctx.enter_context(tc.tile_pool(name="lists", bufs=1))
        held = ctx.enter_context(tc.tile_pool(name="held", bufs=1))
        ring = ctx.enter_context(tc.tile_pool(name="ring", bufs=4))
        psum = ctx.enter_context(tc.psum_pool(name="psum", bufs=1))
        turn = ctx.enter_context(tc.psum_pool(name="turn", bufs=3))

        idx = lists.tile([P, LIST_COLS], U16, name="idx")
        idx2 = lists.tile([P, Q // 16], U16, name="idx2")
        idx3 = lists.tile([P, LIST_COLS], U16, name="idx3")

        key_words = held.tile([P, T], I32, name="key_words")
        key_scales = held.tile([P, T], U8, name="key_scales")
        identity = held.tile([P, P], F32, name="identity")
        user_pairs = [held.tile([P, 2, U], F32, name=f"user_pair{u}") for u in range(2)]
        scale_stage = held.tile([P, T // 4], I32, name="scale_stage")
        factor_stage = held.tile([2, I], F32, name="factor_stage")
        first = [held.tile([P, T], F32, name=f"first{e}") for e in range(E_TILES)]
        second = [held.tile([P, X], F32, name=f"second{e}") for e in range(E_TILES)]

        nc.vector.memset(key_scales[:].bitcast(I32), 0)
        make_identity(nc, identity[:])

        user_rows = users.rearrange("(p u v) c -> u p v c", u=2, v=2)
        scale_rows = keys_scales[0].bitcast(I32).rearrange("(quad r) w -> r quad w", r=4)
        nc.sync.dma_start(key_words[:], keys_words[0].rearrange("p n t -> p (n t)").bitcast(I32))
        nc.sync.dma_start(idx[:], offs)
        for r in range(4):
            nc.sync.dma_start(scale_stage[r:P:32, :], scale_rows[r])
        nc.sync.dma_start(factor_stage[0:1, :], wsc)
        nc.sync.dma_start(user_pairs[0][:], user_rows[0])
        nc.sync.dma_start(factor_stage[1:2, :], vsc)
        nc.sync.dma_start(idx2[:], offs2)
        nc.sync.dma_start(user_pairs[1][:], user_rows[1])
        nc.sync.dma_start(idx3[:], offs3)
        for e in range(E_TILES):
            nc.sync.dma_start(second[e][:], vals2[e * P : (e + 1) * P, :])
            nc.sync.dma_start(first[e][:], vals[e * P : (e + 1) * P, :])

        for quad in range(4):
            rows = slice(32 * quad, 32 * quad + 4)
            nc.vector.tensor_copy(key_scales[rows, :].bitcast(I32), scale_stage[rows, :])
        picked_words = held.tile([P, PACK, P], U32, name="picked_words", align_bytes=64)
        picked_scales = held.tile([P, PACK, P], U8, name="picked_scales", align_bytes=64)
        nc.vector.tensor_copy(dealt(picked_scales), key_scales[:].indirect(idx[:]))
        nc.vector.tensor_copy(dealt(picked_words), key_words[:].bitcast(U32).indirect(idx[:]))

        factor_rows = held.tile([P, PACK, P], F32, name="factor_rows", tag="key_words")
        nc.vector.memset(factor_rows[:], 0.0)
        nc.vector.tensor_copy(dealt(factor_rows)[0:2], listed(factor_stage[:]))
        factor_bank = psum.tile([P, PACK, P], F32, name="factor_bank")
        for t in range(PACK):
            nc.tensor.transpose(factor_bank[:, t, :], factor_rows[:, t, :], identity[:])
        factors = held.tile([P, 2, PACK], F32, name="factors")
        nc.vector.tensor_copy(factors[:], factor_bank[:, :, 0:2].rearrange("p t s -> p s t"))

        queries = held.tile([P, Q, PACK], BF16, name="queries", align_bytes=64)
        picked_users = held.tile([P, PACK, Q], F32, name="picked_users")
        for t in range(PACK):
            nc.scalar.activation(picked_users[:, t, :], user_pairs[t // 2][:, t % 2, :].indirect(idx2[:]), COPY)
        nc.vector.tensor_copy(queries[:], picked_users[:].rearrange("p t q -> p q t"))
        query_codes = held.tile([P, Q], U32, name="query_codes", align_bytes=64)
        query_scales = held.tile([P, Q], U8, name="query_scales", align_bytes=64)
        nc.vector.quantize_mx(
            out=query_codes[:].bitcast(FP8X4),
            scales=query_scales[:],
            in_=queries[:].rearrange("p q t -> p (q t)"),
        )

        score_bank = psum.tile([P, PACK, Q], F32, name="score_bank")
        for t in range(PACK):
            nc.tensor.matmul_mx(
                out=score_bank[:, t, :],
                lhsT=picked_words[:, t, :].bitcast(FP8X4),
                lhsT_scale=picked_scales[:, t, :],
                rhs=query_codes[:].bitcast(FP8X4),
                rhs_scale=query_scales[:],
                start=True,
                stop=True,
            )
        weights = held.tile([P, Q, PACK], BF16, name="weights", align_bytes=64)
        nc.vector.tensor_tensor(
            weights[:],
            score_bank[:].rearrange("p t q -> p q t"),
            factors[:, 0:1, :].to_broadcast([P, Q, PACK]),
            MULT,
        )
        weight_codes = held.tile([P, Q], U32, name="weight_codes", align_bytes=64)
        weight_scales = held.tile([P, Q], U8, name="weight_scales", align_bytes=64)
        nc.vector.quantize_mx(
            out=weight_codes[:].bitcast(FP8X4),
            scales=weight_scales[:],
            in_=weights[:].rearrange("p q t -> p (q t)"),
        )

        early_bank = psum.tile([P, 2 * P], F32, name="early_bank")
        late_banks = [psum.tile([P, P], F32, name=f"late_bank{e}") for e in range(2)]

        def merge_and_turn(e):
            picked_second = ring.tile([P, I], F32, name="picked_second")
            nc.scalar.activation(picked_second[:], second[e][:].indirect(idx3[:]), COPY)
            picked_low = held.tile([P, HALF], F32, name="picked_low", tag="turnstile", align_bytes=64)
            picked_high = ring.tile([P, HALF], F32, name="picked_high")
            nc.vector.tensor_copy(picked_low[:], first[e][:].indirect(idx[:, : LIST_COLS // 2]))
            nc.scalar.activation(picked_high[:], first[e][:].indirect(idx[:, LIST_COLS // 2 :]), COPY)
            larger = ring.tile([P, PACK, P], F32, name="larger")
            low, high = slice(0, BLOCKS // 2), slice(BLOCKS // 2, BLOCKS)
            nc.vector.tensor_tensor(
                dealt(larger)[:, low], listed(picked_low[:]), listed(picked_second[:])[:, low], MAX
            )
            for places in (slice(0, 2), slice(2, 4)):
                nc.vector.tensor_tensor(
                    dealt(larger)[:, high, places],
                    listed(picked_high[:])[:, :, places],
                    listed(picked_second[:])[:, high, places],
                    MAX,
                )
            turned = turn.tile([P, PACK, P], F32, name="turned")
            for t in range(PACK):
                nc.tensor.transpose(turned[:, t, :], larger[:, t, :], identity[:])
            return turned

        def scale_and_multiply(e, turned):
            tag = "turnstile" if e < E_TILES - 2 else f"values{e}"
            values = held.tile([P, P, PACK], BF16, name="values", tag=tag, align_bytes=64)
            nc.vector.tensor_tensor(
                values[:],
                turned[:].rearrange("p t e -> p e t"),
                factors[:, 1:2, :].to_broadcast([P, P, PACK]),
                MULT,
            )
            tag = "turnstile" if e == E_TILES - 2 else f"value_codes{e}"
            value_codes = held.tile([P, P], U32, name="value_codes", tag=tag, align_bytes=64)
            value_scales = ring.tile([P, P], U8, name="value_scales", align_bytes=64)
            nc.vector.quantize_mx(
                out=value_codes[:].bitcast(FP8X4),
                scales=value_scales[:],
                in_=values[:].rearrange("p e t -> p (e t)"),
            )
            nc.tensor.matmul_mx(
                out=early_bank[:, e * P : (e + 1) * P] if e < 2 else late_banks[e - 2][:],
                lhsT=weight_codes[:].bitcast(FP8X4),
                lhsT_scale=weight_scales[:],
                rhs=value_codes[:].bitcast(FP8X4),
                rhs_scale=value_scales[:],
                start=True,
                stop=True,
            )

        turned = merge_and_turn(0)
        for e in range(1, E_TILES):
            ahead = merge_and_turn(e)
            scale_and_multiply(e - 1, turned)
            turned = ahead
        scale_and_multiply(E_TILES - 1, turned)
        early = held.tile([P, 2 * P], F32, name="early", tag=f"first{E_TILES - 1}")
        nc.scalar.activation(early[:], early_bank[:], COPY)
        nc.sync.dma_start(out[:, : 2 * P], early[:])
        for e in range(2, E_TILES):
            late = ring.tile([P, P], F32, name="late")
            nc.scalar.activation(late[:], late_banks[e - 2][:], COPY)
            nc.sync.dma_start(out[:, e * P : (e + 1) * P], late[:])
